import numpy as np
import ml_dtypes


def mxq(x, axis, fmt="e4m3"):
    dtype, down = {"e4m3": (ml_dtypes.float8_e4m3fn, 7), "e5m2": (ml_dtypes.float8_e5m2, 14)}[fmt]
    v = np.moveaxis(np.asarray(x, np.float32).astype(ml_dtypes.bfloat16).astype(np.float64), axis, -1)
    blocks = v.reshape(v.shape[:-1] + (-1, 32))
    amax = np.abs(blocks).max(-1, keepdims=True)
    byte = np.maximum(np.where(amax > 0, np.frexp(amax)[1] - 1 + 127, 0) - down, 1)
    scale = np.exp2(byte - 127.0)
    codes = (blocks / scale).astype(np.float32).astype(dtype).astype(np.float64)
    return np.moveaxis((codes * scale).reshape(v.shape), -1, axis)


WIDE = False


def mx_kscale(k):
    if not WIDE:
        return np.ones(k)
    levels = np.array([10, -10, 5, -5, 0])
    if k % 512:
        return np.exp2(np.random.permutation(np.resize(levels, k // 32))).repeat(32)
    a = np.empty((k // 512, 16))
    for p in range(k // 512):
        a[p, :8] = np.random.permutation(np.resize(levels, 8))
        for g in range(8):
            far = levels[np.abs(levels - a[p, g]) >= 10]
            a[p, g + 8] = far[np.random.randint(len(far))]
    return np.exp2(a.ravel()).repeat(32)


def f64(x):
    return np.asarray(x).astype(np.float64)


def striped(idx):
    return np.tile(np.asarray(idx).reshape(-1, 16).T, (8, 1)).astype(np.uint16)


def unstriped(offs):
    return offs[:16].T.reshape(-1).astype(np.int64)


E2M1 = np.array([0.0, 0.5, 1.0, 1.5, 2.0, 3.0, 4.0, 6.0, -0.0, -0.5, -1.0, -1.5, -2.0, -3.0, -4.0, -6.0])


def pack_weight(w, fmt):
    k, n = w.shape
    w = f64(np.asarray(w, np.float32).astype(ml_dtypes.bfloat16)).reshape(k // 32, 32, n)
    amax = np.abs(w).max(1)
    if fmt == "e4m3":
        byte = np.frexp(amax)[1] - 1 + 127 - 7
    else:
        mant, ex = np.frexp(amax / 6.0)
        byte = np.where(mant > 0.5, ex, ex - 1) + 127
    byte = np.clip(np.where(amax > 0, byte, 1), 1, 254)
    scaled = (w * np.exp2(127.0 - byte)[:, None, :]).reshape(k, n).astype(np.float32)
    by_word = np.ascontiguousarray(scaled.reshape(k // 512, 128, 4, n).transpose(0, 1, 3, 2))
    if fmt == "e4m3":
        words = by_word.astype(ml_dtypes.float8_e4m3fn).view(np.uint8)
    else:
        c = by_word.astype(ml_dtypes.float4_e2m1fn).view(np.uint8) & 0xF
        words = (c[..., 0::2] | (c[..., 1::2] << 4)).reshape(k // 512, 128, 2 * n)
    return np.ascontiguousarray(words), np.ascontiguousarray(byte.astype(np.uint8).reshape(k // 512, 16, n))


def unpack_weight(words, scales, fmt):
    g, _, n = scales.shape
    words = np.ascontiguousarray(words).reshape(g, 128, n, -1)
    if fmt == "e4m3":
        vals = words.view(ml_dtypes.float8_e4m3fn).astype(np.float64)
    else:
        nib = np.empty((g, 128, n, 4), np.uint8)
        nib[..., 0::2] = words & 0xF
        nib[..., 1::2] = words >> 4
        vals = E2M1[nib]
    vals = vals * np.repeat(np.exp2(scales.astype(np.float64) - 127.0), 8, axis=1)[..., None]
    return vals.transpose(0, 1, 3, 2).reshape(g * 512, n)


K, L, T, J, N = 1024, 512, 2048, 512, 512


def setup_inputs():
    n = np.random.standard_normal
    idx = np.random.permutation(T)[:J]
    fk = mx_kscale(K)
    fl = mx_kscale(L)
    xap = pack_weight(n((K, T)) / fk[:, None], "e2m1")
    xbp = pack_weight(n((L, J)) / fl[:, None], "e4m3")
    wbp = pack_weight(n((L, N)) * 1 / np.sqrt(L) * fl[:, None], "e2m1")
    return {
        "xa_words": xap[0],
        "xa_scales": xap[1],
        "wa": (n((K, N)) * 1 / np.sqrt(K) * fk[:, None]).astype(np.float32),
        "xb_words": xbp[0],
        "xb_scales": xbp[1],
        "wb_words": wbp[0],
        "wb_scales": wbp[1],
        "offs": striped(idx),
    }


def reference(xa_words, xa_scales, wa, xb_words, xb_scales, wb_words, wb_scales, offs):
    idx = unstriped(offs)
    xau = unpack_weight(xa_words, xa_scales, "e2m1")
    xbu = unpack_weight(xb_words, xb_scales, "e4m3")
    wbu = unpack_weight(wb_words, wb_scales, "e2m1")
    waq = mxq(f64(wa), 0, "e4m3")
    xaidxg = xau[:, idx]
    p = waq.T @ xaidxg
    q = wbu.T @ xbu
    y = np.maximum(p, q) - 0.25 * (p + q)
    return y

@@ -1,0 +1,220 @@
+from contextlib import ExitStack
+
+import concourse.mybir as mybir
+
+K, L, T, J, N = 1024, 512, 2048, 512, 512
+FLOPS = 2 * (K + L) * N * J
+
+F32 = mybir.dt.float32
+BF16 = mybir.dt.bfloat16
+I32 = mybir.dt.int32
+U32 = mybir.dt.uint32
+U16 = mybir.dt.uint16
+U8 = mybir.dt.uint8
+FP8X4 = mybir.dt.float8_e4m3fn_x4
+FP4X4 = mybir.dt.float4_e2m1fn_x4
+ALU = mybir.AluOpType
+ACT = mybir.ActivationFunctionType
+
+P = 128
+PACK = 4
+K_PASS = P * PACK
+PASSES = K // K_PASS
+TILES = N // P
+
+
+def tile_list_better_of_two_views_kernel(tc, xa_words, xa_scales, wa, xb_words, xb_scales, wb_words, wb_scales, offs, out):
+    nc = tc.nc
+    with ExitStack() as ctx:
+        keep = ctx.enter_context(tc.tile_pool(name="keep", bufs=1))
+        psum = ctx.enter_context(tc.psum_pool(name="psum", bufs=1))
+
+        offsets = keep.tile([P, J // 16], U16, name="offsets")
+        xa_sc = keep.tile([P, PASSES * T], U8, name="xa_sc", align_bytes=64)
+        wb_sc = keep.tile([P, N], U8, name="wb_sc", align_bytes=64)
+        xa_w = {}
+        held = {}
+        got_w = [keep.tile([P, J], U16, name=f"got_w{a}", align_bytes=64) for a in range(PASSES)]
+        got_sc = [keep.tile([P, J], U8, name=f"got_sc{a}", align_bytes=64) for a in range(PASSES)]
+        q_sb = [keep.tile([P, J], F32, name=f"q_sb{t}") for t in range(TILES)]
+        q_ps = [psum.tile([P, J], F32, name=f"q_ps{t}") for t in range(TILES)]
+        s_ps = [psum.tile([P, J], F32, name=f"s_ps{t}") for t in range(TILES)]
+        raw = {}
+        quant = {}
+
+        def load_offs():
+            nc.sync.dma_start(offsets[:], offs)
+
+        def load_xa_sc(eng):
+            src = xa_scales.bitcast(I32).rearrange("a r c -> r a c")
+            dst = xa_sc[:].bitcast(I32).rearrange("p (a c) -> p a c", a=PASSES)
+            for quad in range(4):
+                eng.dma_start(out=dst[32 * quad : 32 * quad + 4], in_=src[4 * quad : 4 * quad + 4])
+
+        def load_plane(eng, scales, plane):
+            src = scales[0].bitcast(I32)
+            dst = plane[:].bitcast(I32)
+            for quad in range(4):
+                eng.dma_start(out=dst[32 * quad : 32 * quad + 4], in_=src[4 * quad : 4 * quad + 4])
+
+        def load_xa(pool, a):
+            xa_w[a] = pool.tile([P, T], U16, name=f"xa_w{a}", align_bytes=64)
+            nc.sync.dma_start(out=xa_w[a][:].bitcast(I32), in_=xa_words[a].bitcast(I32))
+
+        def load_xb(pool):
+            held["xb_w"] = pool.tile([P, J], U32, name="xb_w", align_bytes=64)
+            nc.sync.dma_start(out=held["xb_w"][:].bitcast(I32), in_=xb_words[0].rearrange("p c r -> p (c r)").bitcast(I32))
+
+        def load_wb(pool):
+            held["wb_w"] = pool.tile([P, N], U16, name="wb_w", align_bytes=64)
+            nc.sync.dma_start(out=held["wb_w"][:].bitcast(I32), in_=wb_words[0].bitcast(I32))
+
+        def load_xb_sc(pool, eng):
+            held["xb_sc"] = pool.tile([P, J], U8, name="xb_sc", align_bytes=64)
+            nc.vector.memset(held["xb_sc"][:].bitcast(I32), 0)
+            load_plane(eng, xb_scales, held["xb_sc"])
+
+        def load_wa(pool, tag, a, t0, t1):
+            width = (t1 - t0) * P
+            tile = pool.tile([P, PACK, width], F32, name=f"raw{a}_{t0}", tag=tag)
+            rows = wa[a * K_PASS : (a + 1) * K_PASS, t0 * P : t1 * P]
+            nc.sync.dma_start(out=tile[:], in_=rows.rearrange("(p j) n -> p j n", j=PACK))
+            for t in range(t0, t1):
+                raw[a, t] = tile[:, :, (t - t0) * P : (t - t0 + 1) * P]
+
+        def clock(ap, name):
+            c = keep.tile([P, 1], ap.dtype, name=name)
+            nc.gpsimd.tensor_copy(out=c[:], in_=ap)
+
+        grouped = {}
+
+        def cast(a, t, eng):
+            tile = keep.tile([P, P, PACK], BF16, name=f"grouped{a}_{t}", align_bytes=64)
+            dst = tile[:].rearrange("p (c i) j -> p c j i", i=4)
+            src = raw[a, t].rearrange("p j (c i) -> p c j i", i=4)
+            if eng == "s":
+                nc.scalar.copy(out=dst, in_=src)
+            else:
+                nc.vector.tensor_copy(out=dst, in_=src)
+            grouped[a, t] = tile
+
+        def quantise(a, t):
+            codes = keep.tile([P, P], U32, name=f"codes{a}_{t}", align_bytes=64)
+            scales = keep.tile([P, P], U8, name=f"scales{a}_{t}", align_bytes=64)
+            nc.vector.quantize_mx(out=codes[:].bitcast(FP8X4), scales=scales[:], in_=grouped[a, t][:].rearrange("p c j -> p (c j)"))
+            quant[a, t] = (codes, scales)
+
+        def gather_sc(a):
+            nc.vector.tensor_copy(out=got_sc[a][:], in_=xa_sc[:, a * T : (a + 1) * T].indirect(offsets[:]))
+
+        def gather_w(a):
+            nc.vector.tensor_copy(out=got_w[a][:], in_=xa_w[a][:].indirect(offsets[:]))
+
+        def q_pass(bank, t, stop):
+            nc.tensor.matmul_mx(
+                out=bank[:],
+                lhsT=held["wb_w"][:, t * P : (t + 1) * P].bitcast(FP4X4),
+                lhsT_scale=wb_sc[:, t * P : (t + 1) * P],
+                rhs=held["xb_w"][:].bitcast(FP8X4),
+                rhs_scale=held["xb_sc"][:],
+                start=True,
+                stop=stop,
+            )
+
+        def p_pass(a, t, start, stop):
+            codes, scales = quant[a, t]
+            nc.tensor.matmul_mx(
+                out=s_ps[t][:],
+                lhsT=codes[:].bitcast(FP8X4),
+                lhsT_scale=scales[:],
+                rhs=got_w[a][:].bitcast(FP4X4),
+                rhs_scale=got_sc[a][:],
+                start=start,
+                stop=stop,
+            )
+
+        def q_out(t):
+            nc.scalar.copy(out=q_sb[t][:], in_=q_ps[t][:])
+
+        half = {}
+        res = {}
+
+        def plain_finish(t, c0=0, c1=J):
+            m = keep.tile([P, c1 - c0], F32, name=f"m{t}_{c0}")
+            w = keep.tile([P, c1 - c0], F32, name=f"w{t}_{c0}")
+            r = keep.tile([P, c1 - c0], F32, name=f"r{t}_{c0}")
+            nc.vector.tensor_tensor(out=m[:], in0=s_ps[t][:, c0:c1], in1=q_sb[t][:, c0:c1], op=ALU.max)
+            nc.vector.scalar_tensor_tensor(out=w[:], in0=s_ps[t][:, c0:c1], scalar=-0.25, in1=m[:], op0=ALU.mult, op1=ALU.add)
+            nc.vector.scalar_tensor_tensor(out=r[:], in0=q_sb[t][:, c0:c1], scalar=-0.25, in1=w[:], op0=ALU.mult, op1=ALU.add)
+            nc.sync.dma_start(out=out[t * P : (t + 1) * P, c0:c1], in_=r[:])
+
+        def diff(t, c0=0, c1=J):
+            u = keep.tile([P, c1 - c0], F32, name=f"u{t}_{c0}")
+            a = keep.tile([P, c1 - c0], F32, name=f"a{t}_{c0}")
+            nc.vector.scalar_tensor_tensor(out=u[:], in0=s_ps[t][:, c0:c1], scalar=0.5, in1=q_sb[t][:, c0:c1], op0=ALU.mult, op1=ALU.subtract)
+            nc.scalar.activation(out=a[:], in_=u[:], func=ACT.Abs)
+            half[t, c0] = a
+
+        def finish(t, c0=0, c1=J):
+            r = keep.tile([P, c1 - c0], F32, name=f"r{t}_{c0}")
+            nc.vector.scalar_tensor_tensor(out=r[:], in0=s_ps[t][:, c0:c1], scalar=0.25, in1=half[t, c0][:], op0=ALU.mult, op1=ALU.add)
+            nc.sync.dma_start(out=out[t * P : (t + 1) * P, c0:c1], in_=r[:])
+
+        load_offs()
+        load_wa(keep, "first", 0, 0, 2)
+        load_xa(keep, 0)
+        load_wa(keep, "second", 1, 0, 2)
+        nc.vector.memset(xa_sc[:].bitcast(I32), 0)
+        nc.gpsimd.memset(wb_sc[:].bitcast(I32), 0)
+        load_xa_sc(nc.scalar)
+        load_plane(nc.gpsimd, wb_scales, wb_sc)
+        with tc.tile_pool(name="warm", bufs=1) as early:
+            warm = early.tile([P, 3072], F32, name="warm")
+            nc.vector.memset(warm[:, 3070:3071], 0.0)
+            nc.scalar.activation(out=warm[:, 3071:3072], in_=warm[:, 3070:3071], func=ACT.Abs)
+        late = ctx.enter_context(tc.tile_pool(name="late", bufs=1))
+        load_wb(late)
+        load_xb(late)
+        load_xa(late, 1)
+        load_wa(late, "third", 1, 2, 4)
+        load_xb_sc(late, nc.scalar)
+        gather_sc(0)
+        gather_sc(1)
+        cast(0, 0, "s")
+        cast(0, 1, "s")
+        load_wa(keep, "first", 0, 2, 4)
+        gather_w(0)
+        cast(1, 0, "s")
+        cast(1, 1, "s")
+        quantise(0, 0)
+        quantise(0, 1)
+        quantise(1, 0)
+        quantise(1, 1)
+        p_pass(0, 0, True, False)
+        for t in range(TILES):
+            q_pass(q_ps[t], t, True)
+            q_out(t)
+        for t in range(1, TILES):
+            q_pass(s_ps[t], t, False)
+        p_pass(0, 1, False, False)
+        gather_w(1)
+        p_pass(1, 0, False, True)
+        p_pass(1, 1, False, True)
+        cast(1, 2, "s")
+        cast(1, 3, "s")
+        cast(0, 2, "s")
+        plain_finish(0)
+        diff(1)
+        cast(0, 3, "v")
+        quantise(1, 2)
+        quantise(1, 3)
+        p_pass(1, 2, False, False)
+        p_pass(1, 3, False, False)
+        for t in range(2, 4):
+            quantise(0, t)
+            p_pass(0, t, False, True)
+        finish(1)
+        diff(2)
+        diff(3)
+        finish(2)
+        finish(3)

@@ -21,6 +21,13 @@ PACK = 4
 K_PASS = P * PACK
 PASSES = K // K_PASS
 TILES = N // P
+QUADS = 4
+QUAD = P // QUADS
+ROWS = 4
+LIVE = (QUADS - 1) * QUAD + ROWS
+RUN = 4
+PLAIN = 0
+WARM = 6144
 
 
 def tile_list_better_of_two_views_kernel(tc, xa_words, xa_scales, wa, xb_words, xb_scales, wb_words, wb_scales, offs, out):
@@ -30,191 +37,174 @@ def tile_list_better_of_two_views_kernel(tc, xa_words, xa_scales, wa, xb_words, 
         psum = ctx.enter_context(tc.psum_pool(name="psum", bufs=1))
 
         offsets = keep.tile([P, J // 16], U16, name="offsets")
-        xa_sc = keep.tile([P, PASSES * T], U8, name="xa_sc", align_bytes=64)
-        wb_sc = keep.tile([P, N], U8, name="wb_sc", align_bytes=64)
-        xa_w = {}
-        held = {}
-        got_w = [keep.tile([P, J], U16, name=f"got_w{a}", align_bytes=64) for a in range(PASSES)]
-        got_sc = [keep.tile([P, J], U8, name=f"got_sc{a}", align_bytes=64) for a in range(PASSES)]
-        q_sb = [keep.tile([P, J], F32, name=f"q_sb{t}") for t in range(TILES)]
-        q_ps = [psum.tile([P, J], F32, name=f"q_ps{t}") for t in range(TILES)]
-        s_ps = [psum.tile([P, J], F32, name=f"s_ps{t}") for t in range(TILES)]
-        raw = {}
-        quant = {}
-
-        def load_offs():
-            nc.sync.dma_start(offsets[:], offs)
-
-        def load_xa_sc(eng):
-            src = xa_scales.bitcast(I32).rearrange("a r c -> r a c")
-            dst = xa_sc[:].bitcast(I32).rearrange("p (a c) -> p a c", a=PASSES)
-            for quad in range(4):
-                eng.dma_start(out=dst[32 * quad : 32 * quad + 4], in_=src[4 * quad : 4 * quad + 4])
-
-        def load_plane(eng, scales, plane):
-            src = scales[0].bitcast(I32)
-            dst = plane[:].bitcast(I32)
-            for quad in range(4):
-                eng.dma_start(out=dst[32 * quad : 32 * quad + 4], in_=src[4 * quad : 4 * quad + 4])
+        xa_rows = keep.tile([P, T], U8, name="xa_rows", tag="xa_rows", align_bytes=64)
+        b_planes = keep.tile([P, J + N], U8, name="b_planes", align_bytes=64)
+        picked = [keep.tile([P, J], U16, name=f"picked{a}", align_bytes=64) for a in range(PASSES)]
+        picked_plane = [keep.tile([P, J], U8, name=f"picked_plane{a}", align_bytes=64) for a in range(PASSES)]
+        q_bank = [psum.tile([P, J], F32, name=f"q_bank{t}") for t in range(TILES)]
+        sum_bank = [psum.tile([P, J], F32, name=f"sum_bank{t}") for t in range(TILES)]
+        xa_window, staged, grouped, quantised = {}, {}, {}, {}
+        q_part, left, right = {}, {}, {}
 
         def load_xa(pool, a):
-            xa_w[a] = pool.tile([P, T], U16, name=f"xa_w{a}", align_bytes=64)
-            nc.sync.dma_start(out=xa_w[a][:].bitcast(I32), in_=xa_words[a].bitcast(I32))
-
-        def load_xb(pool):
-            held["xb_w"] = pool.tile([P, J], U32, name="xb_w", align_bytes=64)
-            nc.sync.dma_start(out=held["xb_w"][:].bitcast(I32), in_=xb_words[0].rearrange("p c r -> p (c r)").bitcast(I32))
-
-        def load_wb(pool):
-            held["wb_w"] = pool.tile([P, N], U16, name="wb_w", align_bytes=64)
-            nc.sync.dma_start(out=held["wb_w"][:].bitcast(I32), in_=wb_words[0].bitcast(I32))
-
-        def load_xb_sc(pool, eng):
-            held["xb_sc"] = pool.tile([P, J], U8, name="xb_sc", align_bytes=64)
-            nc.vector.memset(held["xb_sc"][:].bitcast(I32), 0)
-            load_plane(eng, xb_scales, held["xb_sc"])
+            xa_window[a] = pool.tile([P, T], U16, name=f"xa_window{a}", tag=f"xa_window{a}", align_bytes=64)
+            nc.sync.dma_start(out=xa_window[a][:].bitcast(I32), in_=xa_words[a].bitcast(I32))
 
         def load_wa(pool, tag, a, t0, t1):
-            width = (t1 - t0) * P
-            tile = pool.tile([P, PACK, width], F32, name=f"raw{a}_{t0}", tag=tag)
+            tile = pool.tile([P, PACK, (t1 - t0) * P], F32, name=f"staged{a}_{t0}", tag=tag, align_bytes=64)
             rows = wa[a * K_PASS : (a + 1) * K_PASS, t0 * P : t1 * P]
             nc.sync.dma_start(out=tile[:], in_=rows.rearrange("(p j) n -> p j n", j=PACK))
             for t in range(t0, t1):
-                raw[a, t] = tile[:, :, (t - t0) * P : (t - t0 + 1) * P]
+                staged[a, t] = tile[:, :, (t - t0) * P : (t - t0 + 1) * P]
 
-        def clock(ap, name):
-            c = keep.tile([P, 1], ap.dtype, name=name)
-            nc.gpsimd.tensor_copy(out=c[:], in_=ap)
+        def cast_views(a, t):
+            grouped[a, t] = keep.tile([P, P, PACK], BF16, name=f"grouped{a}_{t}", align_bytes=64)
+            dst = grouped[a, t][:].rearrange("p (c i) j -> p c j i", i=RUN)
+            src = staged[a, t].rearrange("p j (c i) -> p c j i", i=RUN)
+            return dst, src
 
-        grouped = {}
-
-        def cast(a, t, eng):
-            tile = keep.tile([P, P, PACK], BF16, name=f"grouped{a}_{t}", align_bytes=64)
-            dst = tile[:].rearrange("p (c i) j -> p c j i", i=4)
-            src = raw[a, t].rearrange("p j (c i) -> p c j i", i=4)
-            if eng == "s":
-                nc.scalar.copy(out=dst, in_=src)
-            else:
-                nc.vector.tensor_copy(out=dst, in_=src)
-            grouped[a, t] = tile
+        def cast(a, t):
+            dst, src = cast_views(a, t)
+            nc.scalar.activation(out=dst, in_=src, func=ACT.Copy, scale=1.0 if t == PLAIN else -1.0)
 
         def quantise(a, t):
             codes = keep.tile([P, P], U32, name=f"codes{a}_{t}", align_bytes=64)
-            scales = keep.tile([P, P], U8, name=f"scales{a}_{t}", align_bytes=64)
-            nc.vector.quantize_mx(out=codes[:].bitcast(FP8X4), scales=scales[:], in_=grouped[a, t][:].rearrange("p c j -> p (c j)"))
-            quant[a, t] = (codes, scales)
+            plane = keep.tile([P, P], U8, name=f"plane{a}_{t}", align_bytes=64)
+            values = grouped[a, t][:].rearrange("p c j -> p (c j)")
+            nc.vector.quantize_mx(out=codes[:].bitcast(FP8X4), scales=plane[:], in_=values)
+            quantised[a, t] = (codes, plane)
 
-        def gather_sc(a):
-            nc.vector.tensor_copy(out=got_sc[a][:], in_=xa_sc[:, a * T : (a + 1) * T].indirect(offsets[:]))
-
-        def gather_w(a):
-            nc.vector.tensor_copy(out=got_w[a][:], in_=xa_w[a][:].indirect(offsets[:]))
+        def gather_words(a):
+            nc.vector.tensor_copy(out=picked[a][:], in_=xa_window[a][:].indirect(offsets[:]))
 
         def q_pass(bank, t, stop):
             nc.tensor.matmul_mx(
                 out=bank[:],
-                lhsT=held["wb_w"][:, t * P : (t + 1) * P].bitcast(FP4X4),
-                lhsT_scale=wb_sc[:, t * P : (t + 1) * P],
-                rhs=held["xb_w"][:].bitcast(FP8X4),
-                rhs_scale=held["xb_sc"][:],
+                lhsT=wb_codes[:, t * P : (t + 1) * P].bitcast(FP4X4),
+                lhsT_scale=b_planes[:, J + t * P : J + (t + 1) * P],
+                rhs=xb_codes[:].bitcast(FP8X4),
+                rhs_scale=b_planes[:, 0:J],
                 start=True,
                 stop=stop,
             )
 
-        def p_pass(a, t, start, stop):
-            codes, scales = quant[a, t]
+        def p_pass(a, t):
+            codes, plane = quantised[a, t]
             nc.tensor.matmul_mx(
-                out=s_ps[t][:],
+                out=sum_bank[t][:],
                 lhsT=codes[:].bitcast(FP8X4),
-                lhsT_scale=scales[:],
-                rhs=got_w[a][:].bitcast(FP4X4),
-                rhs_scale=got_sc[a][:],
-                start=start,
-                stop=stop,
+                lhsT_scale=plane[:],
+                rhs=picked[a][:].bitcast(FP4X4),
+                rhs_scale=picked_plane[a][:],
+                start=(t == PLAIN and a == 0),
+                stop=(a == PASSES - 1),
             )
 
-        def q_out(t):
-            nc.scalar.copy(out=q_sb[t][:], in_=q_ps[t][:])
+        def q_alone(t):
+            q_pass(q_bank[t], t, True)
+            q_part[t] = keep.tile([P, J], F32, name=f"q_part{t}")
+            nc.scalar.activation(out=q_part[t][:], in_=q_bank[t][:], func=ACT.Copy, scale=1.0 if t == PLAIN else 0.5)
 
-        half = {}
-        res = {}
+        def left_term(t, other):
+            left[t] = keep.tile([P, J], F32, name=f"left{t}")
+            nc.vector.scalar_tensor_tensor(out=left[t][:], in0=sum_bank[t][:], scalar=-0.25, in1=other[:], op0=ALU.mult, op1=ALU.add)
 
-        def plain_finish(t, c0=0, c1=J):
-            m = keep.tile([P, c1 - c0], F32, name=f"m{t}_{c0}")
-            w = keep.tile([P, c1 - c0], F32, name=f"w{t}_{c0}")
-            r = keep.tile([P, c1 - c0], F32, name=f"r{t}_{c0}")
-            nc.vector.tensor_tensor(out=m[:], in0=s_ps[t][:, c0:c1], in1=q_sb[t][:, c0:c1], op=ALU.max)
-            nc.vector.scalar_tensor_tensor(out=w[:], in0=s_ps[t][:, c0:c1], scalar=-0.25, in1=m[:], op0=ALU.mult, op1=ALU.add)
-            nc.vector.scalar_tensor_tensor(out=r[:], in0=q_sb[t][:, c0:c1], scalar=-0.25, in1=w[:], op0=ALU.mult, op1=ALU.add)
-            nc.sync.dma_start(out=out[t * P : (t + 1) * P, c0:c1], in_=r[:])
+        def right_term(t, tag):
+            right[t] = keep.tile([P, J], F32, name=f"right{t}", tag=tag, align_bytes=64)
+            nc.scalar.activation(out=right[t][:], in_=sum_bank[t][:], func=ACT.Abs, scale=0.5)
 
-        def diff(t, c0=0, c1=J):
-            u = keep.tile([P, c1 - c0], F32, name=f"u{t}_{c0}")
-            a = keep.tile([P, c1 - c0], F32, name=f"a{t}_{c0}")
-            nc.vector.scalar_tensor_tensor(out=u[:], in0=s_ps[t][:, c0:c1], scalar=0.5, in1=q_sb[t][:, c0:c1], op0=ALU.mult, op1=ALU.subtract)
-            nc.scalar.activation(out=a[:], in_=u[:], func=ACT.Abs)
-            half[t, c0] = a
+        def finish(t, engine, c0, c1):
+            result = keep.tile([P, c1 - c0], F32, name=f"result{t}_{c0}")
+            engine.tensor_tensor(out=result[:], in0=left[t][:, c0:c1], in1=right[t][:, c0:c1], op=ALU.add)
+            nc.sync.dma_start(out=out[t * P : (t + 1) * P, c0:c1], in_=result[:])
 
-        def finish(t, c0=0, c1=J):
-            r = keep.tile([P, c1 - c0], F32, name=f"r{t}_{c0}")
-            nc.vector.scalar_tensor_tensor(out=r[:], in0=s_ps[t][:, c0:c1], scalar=0.25, in1=half[t, c0][:], op0=ALU.mult, op1=ALU.add)
-            nc.sync.dma_start(out=out[t * P : (t + 1) * P, c0:c1], in_=r[:])
-
-        load_offs()
-        load_wa(keep, "first", 0, 0, 2)
+        nc.sync.dma_start(offsets[:], offs)
         load_xa(keep, 0)
-        load_wa(keep, "second", 1, 0, 2)
-        nc.vector.memset(xa_sc[:].bitcast(I32), 0)
-        nc.gpsimd.memset(wb_sc[:].bitcast(I32), 0)
-        load_xa_sc(nc.scalar)
-        load_plane(nc.gpsimd, wb_scales, wb_sc)
+
         with tc.tile_pool(name="warm", bufs=1) as early:
-            warm = early.tile([P, 3072], F32, name="warm")
-            nc.vector.memset(warm[:, 3070:3071], 0.0)
-            nc.scalar.activation(out=warm[:, 3071:3072], in_=warm[:, 3070:3071], func=ACT.Abs)
+            warm = early.tile([P, WARM], F32, name="warm")
+            nc.gpsimd.memset(warm[:, WARM - 2 : WARM - 1], 0.0)
+            nc.scalar.activation(out=warm[:, WARM - 1 : WARM], in_=warm[:, WARM - 2 : WARM - 1], func=ACT.Abs)
+
+        xa_rows_i32 = xa_rows[:].bitcast(I32)
+        b_planes_i32 = b_planes[:].bitcast(I32)
+        nc.vector.memset(xa_rows_i32, 0)
+        nc.gpsimd.memset(b_planes_i32, 0)
+        nc.sync.dma_start(out=b_planes[:, 0:J].bitcast(I32)[0 : QUADS * ROWS], in_=xb_scales[0].bitcast(I32))
+        nc.sync.dma_start(out=b_planes[:, J : J + N].bitcast(I32)[0 : QUADS * ROWS], in_=wb_scales[0].bitcast(I32))
+        for quad in range(QUADS):
+            nc.sync.dma_start(
+                out=xa_rows_i32[QUAD * quad : QUAD * quad + PASSES * ROWS],
+                in_=xa_scales.bitcast(I32)[:, ROWS * quad : ROWS * (quad + 1)],
+            )
+        nc.vector.memset(picked_plane[1][:].bitcast(I32), 0)
+
         late = ctx.enter_context(tc.tile_pool(name="late", bufs=1))
-        load_wb(late)
-        load_xb(late)
+        load_wa(late, "staged0", 0, 0, TILES)
         load_xa(late, 1)
-        load_wa(late, "third", 1, 2, 4)
-        load_xb_sc(late, nc.scalar)
-        gather_sc(0)
-        gather_sc(1)
-        cast(0, 0, "s")
-        cast(0, 1, "s")
-        load_wa(keep, "first", 0, 2, 4)
-        gather_w(0)
-        cast(1, 0, "s")
-        cast(1, 1, "s")
-        quantise(0, 0)
-        quantise(0, 1)
-        quantise(1, 0)
-        quantise(1, 1)
-        p_pass(0, 0, True, False)
+        wb_codes = late.tile([P, N], U16, name="wb_codes", align_bytes=64)
+        nc.sync.dma_start(out=wb_codes[:].bitcast(I32), in_=wb_words[0].bitcast(I32))
+        xb_codes = late.tile([P, J], U32, name="xb_codes", align_bytes=64)
+        nc.sync.dma_start(out=xb_codes[:].bitcast(I32), in_=xb_words[0].rearrange("p c r -> p (c r)").bitcast(I32))
+        for quad in range(1, QUADS):
+            nc.sync.dma_start(
+                out=b_planes_i32[QUAD * quad : QUAD * quad + ROWS],
+                in_=b_planes_i32[ROWS * quad : ROWS * (quad + 1)],
+            )
+
+        gather_words(0)
+        nc.vector.tensor_copy(out=picked_plane[0][:], in_=xa_rows[:].indirect(offsets[:]))
+        load_wa(keep, "xa_window0", 1, 0, TILES // 2)
+        nc.sync.dma_start(
+            out=picked_plane[1][:].bitcast(I32)[0:LIVE],
+            in_=picked_plane[0][:].bitcast(I32)[ROWS : ROWS + LIVE],
+        )
+        load_wa(keep, "xa_rows", 1, TILES // 2, TILES)
+
         for t in range(TILES):
-            q_pass(q_ps[t], t, True)
-            q_out(t)
-        for t in range(1, TILES):
-            q_pass(s_ps[t], t, False)
-        p_pass(0, 1, False, False)
-        gather_w(1)
-        p_pass(1, 0, False, True)
-        p_pass(1, 1, False, True)
-        cast(1, 2, "s")
-        cast(1, 3, "s")
-        cast(0, 2, "s")
-        plain_finish(0)
-        diff(1)
-        cast(0, 3, "v")
-        quantise(1, 2)
-        quantise(1, 3)
-        p_pass(1, 2, False, False)
-        p_pass(1, 3, False, False)
-        for t in range(2, 4):
+            cast(0, t)
+        for t in range(TILES):
             quantise(0, t)
-            p_pass(0, t, False, True)
-        finish(1)
-        diff(2)
-        diff(3)
-        finish(2)
-        finish(3)
+        gather_words(1)
+
+        dst, src = cast_views(1, PLAIN)
+        nc.vector.tensor_scalar(out=dst, in0=src, scalar1=1.0, scalar2=None, op0=ALU.mult)
+        quantise(1, PLAIN)
+        q_alone(PLAIN)
+        right[PLAIN] = keep.tile([P, J], F32, name="right0")
+        nc.gpsimd.tensor_scalar(out=right[PLAIN][:], in0=q_part[PLAIN][:], scalar1=-0.25, scalar2=0.0, op0=ALU.mult, op1=ALU.add)
+        p_pass(0, PLAIN)
+        p_pass(1, PLAIN)
+
+        cast(1, 1)
+        quantise(1, 1)
+        q_alone(1)
+        q_pass(sum_bank[1], 1, False)
+        p_pass(0, 1)
+        p_pass(1, 1)
+
+        last_tiles = range(TILES // 2, TILES)
+        for t in last_tiles:
+            cast(1, t)
+        for t in last_tiles:
+            q_alone(t)
+        for t in last_tiles:
+            q_pass(sum_bank[t], t, False)
+            p_pass(0, t)
+
+        larger = keep.tile([P, J], F32, name="larger")
+        nc.vector.tensor_tensor(out=larger[:], in0=sum_bank[PLAIN][:], in1=q_part[PLAIN][:], op=ALU.max)
+        left_term(PLAIN, larger)
+        finish(PLAIN, nc.gpsimd, 0, J)
+        for t in last_tiles:
+            quantise(1, t)
+            p_pass(1, t)
+        left_term(1, q_part[1])
+        right_term(1, "xa_rows")
+        finish(1, nc.gpsimd, 0, J)
+        for t in last_tiles:
+            left_term(t, q_part[t])
+            right_term(t, f"right{t}")
+        finish(TILES - 2, nc.vector, 0, J)
+        finish(TILES - 1, nc.vector, 0, J // 2)
+        finish(TILES - 1, nc.vector, J // 2, J)

from contextlib import ExitStack

import concourse.mybir as mybir

K, L, T, J, N = 1024, 512, 2048, 512, 512
FLOPS = 2 * (K + L) * N * J

F32 = mybir.dt.float32
BF16 = mybir.dt.bfloat16
I32 = mybir.dt.int32
U32 = mybir.dt.uint32
U16 = mybir.dt.uint16
U8 = mybir.dt.uint8
FP8X4 = mybir.dt.float8_e4m3fn_x4
FP4X4 = mybir.dt.float4_e2m1fn_x4
ALU = mybir.AluOpType
ACT = mybir.ActivationFunctionType

P = 128
PACK = 4
K_PASS = P * PACK
PASSES = K // K_PASS
TILES = N // P
QUADS = 4
QUAD = P // QUADS
ROWS = 4
LIVE = (QUADS - 1) * QUAD + ROWS
RUN = 4
PLAIN = 0
WARM = 6144


def tile_list_better_of_two_views_kernel(tc, xa_words, xa_scales, wa, xb_words, xb_scales, wb_words, wb_scales, offs, out):
    nc = tc.nc
    with ExitStack() as ctx:
        keep = ctx.enter_context(tc.tile_pool(name="keep", bufs=1))
        psum = ctx.enter_context(tc.psum_pool(name="psum", bufs=1))

        offsets = keep.tile([P, J // 16], U16, name="offsets")
        xa_rows = keep.tile([P, T], U8, name="xa_rows", tag="xa_rows", align_bytes=64)
        b_planes = keep.tile([P, J + N], U8, name="b_planes", align_bytes=64)
        picked = [keep.tile([P, J], U16, name=f"picked{a}", align_bytes=64) for a in range(PASSES)]
        picked_plane = [keep.tile([P, J], U8, name=f"picked_plane{a}", align_bytes=64) for a in range(PASSES)]
        q_bank = [psum.tile([P, J], F32, name=f"q_bank{t}") for t in range(TILES)]
        sum_bank = [psum.tile([P, J], F32, name=f"sum_bank{t}") for t in range(TILES)]
        xa_window, staged, grouped, quantised = {}, {}, {}, {}
        q_part, left, right = {}, {}, {}

        def load_xa(pool, a):
            xa_window[a] = pool.tile([P, T], U16, name=f"xa_window{a}", tag=f"xa_window{a}", align_bytes=64)
            nc.sync.dma_start(out=xa_window[a][:].bitcast(I32), in_=xa_words[a].bitcast(I32))

        def load_wa(pool, tag, a, t0, t1):
            tile = pool.tile([P, PACK, (t1 - t0) * P], F32, name=f"staged{a}_{t0}", tag=tag, align_bytes=64)
            rows = wa[a * K_PASS : (a + 1) * K_PASS, t0 * P : t1 * P]
            nc.sync.dma_start(out=tile[:], in_=rows.rearrange("(p j) n -> p j n", j=PACK))
            for t in range(t0, t1):
                staged[a, t] = tile[:, :, (t - t0) * P : (t - t0 + 1) * P]

        def cast_views(a, t):
            grouped[a, t] = keep.tile([P, P, PACK], BF16, name=f"grouped{a}_{t}", align_bytes=64)
            dst = grouped[a, t][:].rearrange("p (c i) j -> p c j i", i=RUN)
            src = staged[a, t].rearrange("p j (c i) -> p c j i", i=RUN)
            return dst, src

        def cast(a, t):
            dst, src = cast_views(a, t)
            nc.scalar.activation(out=dst, in_=src, func=ACT.Copy, scale=1.0 if t == PLAIN else -1.0)

        def quantise(a, t):
            codes = keep.tile([P, P], U32, name=f"codes{a}_{t}", align_bytes=64)
            plane = keep.tile([P, P], U8, name=f"plane{a}_{t}", align_bytes=64)
            values = grouped[a, t][:].rearrange("p c j -> p (c j)")
            nc.vector.quantize_mx(out=codes[:].bitcast(FP8X4), scales=plane[:], in_=values)
            quantised[a, t] = (codes, plane)

        def gather_words(a):
            nc.vector.tensor_copy(out=picked[a][:], in_=xa_window[a][:].indirect(offsets[:]))

        def q_pass(bank, t, stop):
            nc.tensor.matmul_mx(
                out=bank[:],
                lhsT=wb_codes[:, t * P : (t + 1) * P].bitcast(FP4X4),
                lhsT_scale=b_planes[:, J + t * P : J + (t + 1) * P],
                rhs=xb_codes[:].bitcast(FP8X4),
                rhs_scale=b_planes[:, 0:J],
                start=True,
                stop=stop,
            )

        def p_pass(a, t):
            codes, plane = quantised[a, t]
            nc.tensor.matmul_mx(
                out=sum_bank[t][:],
                lhsT=codes[:].bitcast(FP8X4),
                lhsT_scale=plane[:],
                rhs=picked[a][:].bitcast(FP4X4),
                rhs_scale=picked_plane[a][:],
                start=(t == PLAIN and a == 0),
                stop=(a == PASSES - 1),
            )

        def q_alone(t):
            q_pass(q_bank[t], t, True)
            q_part[t] = keep.tile([P, J], F32, name=f"q_part{t}")
            nc.scalar.activation(out=q_part[t][:], in_=q_bank[t][:], func=ACT.Copy, scale=1.0 if t == PLAIN else 0.5)

        def left_term(t, other):
            left[t] = keep.tile([P, J], F32, name=f"left{t}")
            nc.vector.scalar_tensor_tensor(out=left[t][:], in0=sum_bank[t][:], scalar=-0.25, in1=other[:], op0=ALU.mult, op1=ALU.add)

        def right_term(t, tag):
            right[t] = keep.tile([P, J], F32, name=f"right{t}", tag=tag, align_bytes=64)
            nc.scalar.activation(out=right[t][:], in_=sum_bank[t][:], func=ACT.Abs, scale=0.5)

        def finish(t, engine, c0, c1):
            result = keep.tile([P, c1 - c0], F32, name=f"result{t}_{c0}")
            engine.tensor_tensor(out=result[:], in0=left[t][:, c0:c1], in1=right[t][:, c0:c1], op=ALU.add)
            nc.sync.dma_start(out=out[t * P : (t + 1) * P, c0:c1], in_=result[:])

        nc.sync.dma_start(offsets[:], offs)
        load_xa(keep, 0)

        with tc.tile_pool(name="warm", bufs=1) as early:
            warm = early.tile([P, WARM], F32, name="warm")
            nc.gpsimd.memset(warm[:, WARM - 2 : WARM - 1], 0.0)
            nc.scalar.activation(out=warm[:, WARM - 1 : WARM], in_=warm[:, WARM - 2 : WARM - 1], func=ACT.Abs)

        xa_rows_i32 = xa_rows[:].bitcast(I32)
        b_planes_i32 = b_planes[:].bitcast(I32)
        nc.vector.memset(xa_rows_i32, 0)
        nc.gpsimd.memset(b_planes_i32, 0)
        nc.sync.dma_start(out=b_planes[:, 0:J].bitcast(I32)[0 : QUADS * ROWS], in_=xb_scales[0].bitcast(I32))
        nc.sync.dma_start(out=b_planes[:, J : J + N].bitcast(I32)[0 : QUADS * ROWS], in_=wb_scales[0].bitcast(I32))
        for quad in range(QUADS):
            nc.sync.dma_start(
                out=xa_rows_i32[QUAD * quad : QUAD * quad + PASSES * ROWS],
                in_=xa_scales.bitcast(I32)[:, ROWS * quad : ROWS * (quad + 1)],
            )
        nc.vector.memset(picked_plane[1][:].bitcast(I32), 0)

        late = ctx.enter_context(tc.tile_pool(name="late", bufs=1))
        load_wa(late, "staged0", 0, 0, TILES)
        load_xa(late, 1)
        wb_codes = late.tile([P, N], U16, name="wb_codes", align_bytes=64)
        nc.sync.dma_start(out=wb_codes[:].bitcast(I32), in_=wb_words[0].bitcast(I32))
        xb_codes = late.tile([P, J], U32, name="xb_codes", align_bytes=64)
        nc.sync.dma_start(out=xb_codes[:].bitcast(I32), in_=xb_words[0].rearrange("p c r -> p (c r)").bitcast(I32))
        for quad in range(1, QUADS):
            nc.sync.dma_start(
                out=b_planes_i32[QUAD * quad : QUAD * quad + ROWS],
                in_=b_planes_i32[ROWS * quad : ROWS * (quad + 1)],
            )

        gather_words(0)
        nc.vector.tensor_copy(out=picked_plane[0][:], in_=xa_rows[:].indirect(offsets[:]))
        load_wa(keep, "xa_window0", 1, 0, TILES // 2)
        nc.sync.dma_start(
            out=picked_plane[1][:].bitcast(I32)[0:LIVE],
            in_=picked_plane[0][:].bitcast(I32)[ROWS : ROWS + LIVE],
        )
        load_wa(keep, "xa_rows", 1, TILES // 2, TILES)

        for t in range(TILES):
            cast(0, t)
        for t in range(TILES):
            quantise(0, t)
        gather_words(1)

        dst, src = cast_views(1, PLAIN)
        nc.vector.tensor_scalar(out=dst, in0=src, scalar1=1.0, scalar2=None, op0=ALU.mult)
        quantise(1, PLAIN)
        q_alone(PLAIN)
        right[PLAIN] = keep.tile([P, J], F32, name="right0")
        nc.gpsimd.tensor_scalar(out=right[PLAIN][:], in0=q_part[PLAIN][:], scalar1=-0.25, scalar2=0.0, op0=ALU.mult, op1=ALU.add)
        p_pass(0, PLAIN)
        p_pass(1, PLAIN)

        cast(1, 1)
        quantise(1, 1)
        q_alone(1)
        q_pass(sum_bank[1], 1, False)
        p_pass(0, 1)
        p_pass(1, 1)

        last_tiles = range(TILES // 2, TILES)
        for t in last_tiles:
            cast(1, t)
        for t in last_tiles:
            q_alone(t)
        for t in last_tiles:
            q_pass(sum_bank[t], t, False)
            p_pass(0, t)

        larger = keep.tile([P, J], F32, name="larger")
        nc.vector.tensor_tensor(out=larger[:], in0=sum_bank[PLAIN][:], in1=q_part[PLAIN][:], op=ALU.max)
        left_term(PLAIN, larger)
        finish(PLAIN, nc.gpsimd, 0, J)
        for t in last_tiles:
            quantise(1, t)
            p_pass(1, t)
        left_term(1, q_part[1])
        right_term(1, "xa_rows")
        finish(1, nc.gpsimd, 0, J)
        for t in last_tiles:
            left_term(t, q_part[t])
            right_term(t, f"right{t}")
        finish(TILES - 2, nc.vector, 0, J)
        finish(TILES - 1, nc.vector, 0, J // 2)
        finish(TILES - 1, nc.vector, J // 2, J)
